import numpy as np
import ml_dtypes


def mxq(x, axis, fmt="e4m3"):
    dtype, down = {"e4m3": (ml_dtypes.float8_e4m3fn, 7), "e5m2": (ml_dtypes.float8_e5m2, 14)}[fmt]
    v = np.moveaxis(np.asarray(x, np.float32).astype(ml_dtypes.bfloat16).astype(np.float64), axis, -1)
    blocks = v.reshape(v.shape[:-1] + (-1, 32))
    amax = np.abs(blocks).max(-1, keepdims=True)
    byte = np.maximum(np.where(amax > 0, np.frexp(amax)[1] - 1 + 127, 0) - down, 1)
    scale = np.exp2(byte - 127.0)
    codes = (blocks / scale).astype(np.float32).astype(dtype).astype(np.float64)
    return np.moveaxis((codes * scale).reshape(v.shape), -1, axis)


WIDE = False


def mx_kscale(k):
    if not WIDE:
        return np.ones(k)
    levels = np.array([10, -10, 5, -5, 0])
    if k % 512:
        return np.exp2(np.random.permutation(np.resize(levels, k // 32))).repeat(32)
    a = np.empty((k // 512, 16))
    for p in range(k // 512):
        a[p, :8] = np.random.permutation(np.resize(levels, 8))
        for g in range(8):
            far = levels[np.abs(levels - a[p, g]) >= 10]
            a[p, g + 8] = far[np.random.randint(len(far))]
    return np.exp2(a.ravel()).repeat(32)


def f64(x):
    return np.asarray(x).astype(np.float64)


def striped(idx):
    return np.tile(idx.reshape(-1, 16).T, (8, 1)).astype(np.uint16)


def unstriped(offs):
    return offs[:16].T.reshape(-1).astype(np.int64)


def pack_weight(w):
    k, n = w.shape
    w = f64(np.asarray(w, np.float32).astype(ml_dtypes.bfloat16)).reshape(k // 32, 32, n)
    amax = np.abs(w).max(1)
    byte = np.clip(np.where(amax > 0, np.frexp(amax)[1] - 1 + 127 - 7, 1), 1, 254)
    scaled = (w * np.exp2(127.0 - byte)[:, None, :]).reshape(k, n).astype(np.float32)
    words = np.ascontiguousarray(scaled.reshape(k // 512, 128, 4, n).transpose(0, 1, 3, 2)).astype(ml_dtypes.float8_e4m3fn).view(np.uint8)
    return words, np.ascontiguousarray(byte.astype(np.uint8).reshape(k // 512, 16, n))


def unpack_weight(words, scales):
    g, p, n, _ = words.shape
    vals = np.ascontiguousarray(words).view(ml_dtypes.float8_e4m3fn).astype(np.float64) * np.repeat(np.exp2(scales.astype(np.float64) - 127.0), 8, axis=1)[..., None]
    return vals.transpose(0, 1, 3, 2).reshape(g * 512, n)

def planes(y):
    n, m = y.shape
    v = y.astype(np.float32).astype(ml_dtypes.bfloat16).astype(np.float64).reshape(n // 32, 32, m)
    top = np.abs(v).max(1)
    byte = np.clip(np.where(top > 0, np.frexp(top)[1] - 1 + 127 - 7, 1), 1, 254)
    codes = (v * np.exp2(127.0 - byte)[:, None, :]).reshape(n, m).astype(np.float32).astype(ml_dtypes.float8_e4m3fn).view(np.uint8)
    words = codes.reshape(n // 512, 128, 4, m).transpose(0, 1, 3, 2)
    return np.ascontiguousarray(words), np.ascontiguousarray(byte.astype(np.uint8).reshape(n // 512, 16, m))


K, T, S, H = 512, 1024, 512, 512


def setup_inputs():
    n = np.random.standard_normal
    s = mx_kscale(K)[:, None]
    u = mx_kscale(H)
    packed_xT = pack_weight(n((K, T)) * s)
    return {
        "x_words": packed_xT[0],
        "x_scales": packed_xT[1],
        "w1": (n((K, H)) / np.sqrt(K) / s).astype(np.float32),
        "w2": (n((H, H)) / np.sqrt(H) / u[:, None]).astype(np.float32),
        "gamma": (np.random.uniform(0.5, 1.5, (H, 1)) * u[:, None]).astype(np.float32),
        "offs": striped(np.random.permutation(T)[:S]),
    }


def reference(x_words, x_scales, w1, w2, gamma, offs):
    xq = unpack_weight(x_words, x_scales)[:, unstriped(offs)]
    h = mxq(f64(w1), 0, "e4m3").T @ xq
    hn = (h - h.mean(axis=1, keepdims=True)) / np.sqrt(h.var(axis=1, keepdims=True) + 1e-5)
    z = f64(gamma) * hn
    out_0 = mxq(f64(w2), 0, "e4m3").T @ mxq(z, 0, "e4m3")
    return (out_0,) + planes(out_0)

@@ -1,0 +1,252 @@
+from contextlib import ExitStack
+
+import concourse.mybir as mybir
+
+F32 = mybir.dt.float32
+BF16 = mybir.dt.bfloat16
+I32 = mybir.dt.int32
+U32 = mybir.dt.uint32
+U16 = mybir.dt.uint16
+U8 = mybir.dt.uint8
+FP8X4 = mybir.dt.float8_e4m3fn_x4
+ACT = mybir.ActivationFunctionType
+ALU = mybir.AluOpType
+
+P = 128
+PACK = 4
+T = 1024
+S = 512
+H = 512
+HALF = S // 2
+CH = S // 4
+EPS = 1e-5
+
+FLOPS = 2 * 2 * 512 * 512 * 512
+
+
+def tile_picked_inorm_none_po_kernel(
+    tc, x_words, x_scales, w1, w2, gamma, offs, out_0, out_1, out_2
+):
+    nc = tc.nc
+    with ExitStack() as ctx:
+        sb = ctx.enter_context(tc.tile_pool(name="sb", bufs=1))
+        ps = ctx.enter_context(tc.psum_pool(name="ps", bufs=1))
+
+        def tile(name, shape, dtype):
+            return sb.tile(shape, dtype, name=name, align_bytes=64)
+
+        offsets = sb.tile([P, S // 16], U16, name="offsets")
+        xw = tile("xw", [P, T], U32)
+        xs = tile("xs", [P, T], U8)
+        w1_raw = tile("w1_raw", [P, PACK, H], F32)
+        w2_raw = [tile("w2_raw%d" % h, [P, PACK, H // 2], F32) for h in range(2)]
+        gam = tile("gam", [P, PACK], F32)
+        warm = tile("warm", [P, 2], F32)
+
+        nc.vector.memset(xs[:].bitcast(I32), 0)
+        nc.vector.memset(warm[:, 0:1], 1.0)
+        nc.scalar.activation(warm[:, 1:2], warm[:, 0:1], ACT.Abs_reciprocal_sqrt, bias=EPS)
+
+        nc.sync.dma_start(offsets[:], offs)
+        nc.sync.dma_start(xw[:].bitcast(I32), x_words[0].rearrange("p c r -> p (c r)").bitcast(I32))
+        for q in range(4):
+            nc.sync.dma_start(
+                xs[32 * q : 32 * q + 4, :].bitcast(I32), x_scales[0, 4 * q : 4 * q + 4, :].bitcast(I32)
+            )
+        nc.sync.dma_start(w1_raw[:], w1.rearrange("(p j) n -> p j n", j=PACK))
+        nc.sync.dma_start(gam[:], gamma.rearrange("(p t) o -> p (t o)", t=PACK))
+        w2_rows = w2.rearrange("(p j) n -> p j n", j=PACK)
+        for h in range(2):
+            nc.sync.dma_start(w2_raw[h][:], w2_rows[:, :, h * (H // 2) : (h + 1) * (H // 2)])
+
+        xg = tile("xg", [P, S], U32)
+        xsg = tile("xsg", [P, S], U8)
+        nc.vector.tensor_copy(xg[:], xw[:].indirect(offsets[:]))
+        nc.vector.tensor_copy(xsg[:], xs[:].indirect(offsets[:]))
+
+        w1_src = w1_raw[:].rearrange("p j (m t) -> p m j t", t=PACK)
+        w1_b = [tile("w1_b%d" % a, [P, 2, P, PACK], BF16) for a in range(2)]
+        w1_c = [tile("w1_c%d" % t, [P, P], U32) for t in range(PACK)]
+        w1_s = [tile("w1_s%d" % t, [P, P], U8) for t in range(PACK)]
+
+        def cast_w1(copy, a, m0, m1):
+            copy(w1_b[a][:].rearrange("p t m j -> p m j t")[:, m0:m1], w1_src[:, m0:m1, :, 2 * a : 2 * a + 2])
+
+        def quant_w1(t):
+            nc.vector.quantize_mx(
+                out=w1_c[t][:].bitcast(FP8X4),
+                scales=w1_s[t][:],
+                in_=w1_b[t // 2][:, t % 2].rearrange("p m j -> p (m j)"),
+            )
+
+        cast_w1(nc.vector.tensor_copy, 0, 0, 72)
+        cast_w1(nc.scalar.copy, 0, 72, P)
+        cast_w1(nc.vector.tensor_copy, 1, 0, 40)
+        cast_w1(nc.scalar.copy, 1, 80, P)
+
+        u = tile("u", [P, PACK, 2], F32)
+        stats = tile("stats", [P, PACK - 1, 12], F32)
+        neg_gam = tile("neg_gam", [P, PACK], F32)
+        mv = tile("mv", [P, PACK, 2], F32)
+        rstd = tile("rstd", [P, PACK], F32)
+        coef = tile("coef", [P, PACK, 2], F32)
+        zt = [tile("zt%d" % h, [P, PACK, HALF], BF16) for h in range(2)]
+        w2_b = tile("w2_b", [P, PACK, P, PACK], BF16)
+        w2_c = tile("w2_c", [P, H], U32)
+        w2_s = tile("w2_s", [P, H], U8)
+
+        def cast_w2(copy, h, m0, m1):
+            copy(
+                w2_b[:].rearrange("p t m j -> p m j t")[:, h * 64 + m0 : h * 64 + m1],
+                w2_raw[h][:].rearrange("p j (m t) -> p m j t", t=PACK)[:, m0:m1],
+            )
+
+        last_stats = w2_b[:, PACK - 1].rearrange("p m j -> p (m j)").bitcast(F32)[:, 240:252]
+
+        hb = [[None, None] for t in range(PACK)]
+
+        def project(t):
+            for h in range(2):
+                cols = slice(h * HALF, (h + 1) * HALF)
+                hb[t][h] = ps.tile([P, HALF], F32, name="h%d%d" % (t, h), tag="bank%d%d" % (t, h))
+                nc.tensor.matmul_mx(
+                    out=hb[t][h][:],
+                    lhsT=w1_c[t][:].bitcast(FP8X4),
+                    lhsT_scale=w1_s[t][:],
+                    rhs=xg[:, cols].bitcast(FP8X4),
+                    rhs_scale=xsg[:, cols],
+                    start=True,
+                    stop=True,
+                )
+
+        def moments(t, h):
+            st = last_stats if t == PACK - 1 else stats[:, t, :]
+            nc.vector.bn_stats(st[:, 6 * h : 6 * h + 6], hb[t][h][:])
+
+        def aggregate(t):
+            nc.vector.bn_aggr(mv[:, t, :], last_stats if t == PACK - 1 else stats[:, t, :])
+
+        def inverse_deviation(t):
+            nc.scalar.activation(rstd[:, t : t + 1], mv[:, t, 1:2], ACT.Abs_reciprocal_sqrt, bias=EPS)
+            nc.scalar.activation(u[:, t, 1:2], mv[:, t, 0:1], ACT.Copy, scale=neg_gam[:, t : t + 1])
+
+        def coefficients(t):
+            nc.scalar.activation(coef[:, t, :], u[:, t, :], ACT.Copy, scale=rstd[:, t : t + 1])
+
+        def normalise(t, h, c0, c1):
+            nc.scalar.activation(
+                zt[h][:, t, c0:c1], hb[t][h][:, c0:c1], ACT.Identity, bias=coef[:, t, 1:2], scale=coef[:, t, 0:1]
+            )
+
+        quant_w1(0)
+        quant_w1(1)
+        cast_w1(nc.vector.tensor_copy, 1, 40, 80)
+        quant_w1(2)
+        quant_w1(3)
+        nc.scalar.activation(u[:, :, 0], gam[:], ACT.Copy)
+        nc.scalar.activation(neg_gam[:], gam[:], ACT.Copy, scale=-1.0)
+        for t in range(PACK):
+            project(t)
+        cast_w2(nc.scalar.copy, 0, 0, 64)
+        moments(0, 0)
+        for t in range(PACK):
+            moments(t, 1)
+            if t + 1 < PACK:
+                moments(t + 1, 0)
+            aggregate(t)
+            inverse_deviation(t)
+            if t > 0:
+                normalise(t - 1, 0, 0, HALF)
+            coefficients(t)
+            if t > 0:
+                normalise(t - 1, 1, 0, HALF)
+        cast_w2(nc.vector.tensor_copy, 1, 0, 64)
+        nc.vector.quantize_mx(
+            out=w2_c[:].bitcast(FP8X4), scales=w2_s[:], in_=w2_b[:].rearrange("p t m j -> p (t m j)")
+        )
+        normalise(3, 0, 0, CH)
+        normalise(3, 0, CH, HALF)
+        normalise(3, 1, 0, HALF)
+
+        def weave(copy, dst, src):
+            copy(dst.rearrange("p (c i) t -> p c t i", i=4), src.rearrange("p t (c i) -> p c t i", i=4))
+
+        z_b = [tile("z_b%d" % c, [P, CH, PACK], BF16) for c in range(4)]
+        z_c = [tile("z_c%d" % c, [P, CH], U32) for c in range(4)]
+        z_s = [tile("z_s%d" % c, [P, CH], U8) for c in range(4)]
+        y = [tile("y%d" % h, [P, PACK, HALF], F32) for h in range(2)]
+        y_b = [tile("y_b%d" % h, [P, HALF, PACK], BF16) for h in range(2)]
+        y_c = tile("y_c", [P, S], U32)
+        y_s = tile("y_s", [P, S], U8)
+        out_rows = out_0.rearrange("(p t) n -> p t n", t=PACK)
+        out_words = out_1[0].rearrange("p c r -> p (c r)").bitcast(I32)
+
+        def within(c):
+            return slice((c % 2) * CH, (c % 2 + 1) * CH)
+
+        def weave_z(copy, c):
+            weave(copy, z_b[c][:], zt[c // 2][:, :, within(c)])
+
+        def quant_z(c):
+            nc.vector.quantize_mx(
+                out=z_c[c][:].bitcast(FP8X4), scales=z_s[c][:], in_=z_b[c][:].rearrange("p n t -> p (n t)")
+            )
+
+        def second(c):
+            h = c // 2
+            for a in range(2):
+                acc = ps.tile([P, 2, CH], F32, name="y%d%d" % (c, a), tag="bank%d%d" % (2 * (c % 2) + a, h))
+                for e in range(2):
+                    t = 2 * a + e
+                    nc.tensor.matmul_mx(
+                        out=acc[:, e, :],
+                        lhsT=w2_c[:, t * P : (t + 1) * P].bitcast(FP8X4),
+                        lhsT_scale=w2_s[:, t * P : (t + 1) * P],
+                        rhs=z_c[c][:].bitcast(FP8X4),
+                        rhs_scale=z_s[c][:],
+                        start=True,
+                        stop=True,
+                    )
+                nc.scalar.copy(y[h][:, 2 * a : 2 * a + 2, within(c)], acc[:])
+            if c % 2 == 1:
+                nc.sync.dma_start(out_rows[:, :, h * HALF : (h + 1) * HALF], y[h][:])
+
+        def weave_y(c):
+            weave(nc.vector.tensor_copy, y_b[c // 2][:, within(c), :], y[c // 2][:, :, within(c)])
+
+        def planes(c0, c1):
+            cols = slice(c0 * CH, c1 * CH)
+            h = c0 // 2
+            nc.vector.quantize_mx(
+                out=y_c[:, cols].bitcast(FP8X4),
+                scales=y_s[:, cols],
+                in_=y_b[h][:, c0 * CH - h * HALF : c1 * CH - h * HALF, :].rearrange("p n t -> p (n t)"),
+            )
+            if c1 % 2 == 0:
+                half = slice(h * HALF, (h + 1) * HALF)
+                nc.sync.dma_start(out_words[:, half], y_c[:, half].bitcast(I32))
+
+        weave_z(nc.vector.tensor_copy, 0)
+        weave_z(nc.scalar.copy, 3)
+        quant_z(0)
+        weave_z(nc.vector.tensor_copy, 1)
+        second(0)
+        quant_z(1)
+        weave_z(nc.vector.tensor_copy, 2)
+        second(1)
+        quant_z(2)
+        quant_z(3)
+        second(2)
+        second(3)
+        weave_y(0)
+        weave_y(1)
+        planes(0, 2)
+        weave_y(2)
+        planes(2, 3)
+        weave_y(3)
+        planes(3, 4)
+        for q in range(4):
+            queue = nc.sync if q < 2 else nc.scalar
+            queue.dma_start(
+                out_2[0, 4 * q : 4 * q + 4, :].bitcast(I32), y_s[32 * q : 32 * q + 4, :].bitcast(I32)
+            )

@@ -84,13 +84,13 @@ def tile_picked_inorm_none_po_kernel(
         cast_w1(nc.vector.tensor_copy, 1, 0, 40)
         cast_w1(nc.scalar.copy, 1, 80, P)
 
-        u = tile("u", [P, PACK, 2], F32)
-        stats = tile("stats", [P, PACK - 1, 12], F32)
+        u = sb.tile([P, PACK, 2], F32, name="u", tag="late", align_bytes=64)
+        early_stats = tile("early_stats", [P, 2, 12], F32)
         neg_gam = tile("neg_gam", [P, PACK], F32)
         mv = tile("mv", [P, PACK, 2], F32)
         rstd = tile("rstd", [P, PACK], F32)
         coef = tile("coef", [P, PACK, 2], F32)
-        zt = [tile("zt%d" % h, [P, PACK, HALF], BF16) for h in range(2)]
+        zt = [tile("zt0", [P, PACK, HALF], BF16)]
         w2_b = tile("w2_b", [P, PACK, P, PACK], BF16)
         w2_c = tile("w2_c", [P, H], U32)
         w2_s = tile("w2_s", [P, H], U8)
@@ -101,7 +101,23 @@ def tile_picked_inorm_none_po_kernel(
                 w2_raw[h][:].rearrange("p j (m t) -> p m j t", t=PACK)[:, m0:m1],
             )
 
-        last_stats = w2_b[:, PACK - 1].rearrange("p m j -> p (m j)").bitcast(F32)[:, 240:252]
+        def cast_w2_late(a):
+            nc.vector.tensor_copy(
+                w2_b[:].rearrange("p t m j -> p m j t")[:, 64:128, :, 2 * a : 2 * a + 2],
+                w2_raw[1][:].rearrange("p j (m t) -> p m j t", t=PACK)[:, :, :, 2 * a : 2 * a + 2],
+            )
+
+        def quant_w2(a):
+            cols = slice(2 * a * P, 2 * (a + 1) * P)
+            nc.vector.quantize_mx(
+                out=w2_c[:, cols].bitcast(FP8X4),
+                scales=w2_s[:, cols],
+                in_=w2_b[:, 2 * a : 2 * a + 2].rearrange("p t m j -> p (t m j)"),
+            )
+
+        stats = [early_stats[:, 0, :], early_stats[:, 1, :]] + [
+            w2_b[:, t].rearrange("p m j -> p (m j)").bitcast(F32)[:, 240:252] for t in (1, 3)
+        ]
 
         hb = [[None, None] for t in range(PACK)]
 
@@ -120,11 +136,10 @@ def tile_picked_inorm_none_po_kernel(
                 )
 
         def moments(t, h):
-            st = last_stats if t == PACK - 1 else stats[:, t, :]
-            nc.vector.bn_stats(st[:, 6 * h : 6 * h + 6], hb[t][h][:])
+            nc.vector.bn_stats(stats[t][:, 6 * h : 6 * h + 6], hb[t][h][:])
 
         def aggregate(t):
-            nc.vector.bn_aggr(mv[:, t, :], last_stats if t == PACK - 1 else stats[:, t, :])
+            nc.vector.bn_aggr(mv[:, t, :], stats[t])
 
         def inverse_deviation(t):
             nc.scalar.activation(rstd[:, t : t + 1], mv[:, t, 1:2], ACT.Abs_reciprocal_sqrt, bias=EPS)
@@ -148,25 +163,23 @@ def tile_picked_inorm_none_po_kernel(
         for t in range(PACK):
             project(t)
         cast_w2(nc.scalar.copy, 0, 0, 64)
-        moments(0, 0)
         for t in range(PACK):
+            moments(t, 0)
             moments(t, 1)
-            if t + 1 < PACK:
-                moments(t + 1, 0)
             aggregate(t)
             inverse_deviation(t)
             if t > 0:
                 normalise(t - 1, 0, 0, HALF)
             coefficients(t)
-            if t > 0:
-                normalise(t - 1, 1, 0, HALF)
-        cast_w2(nc.vector.tensor_copy, 1, 0, 64)
-        nc.vector.quantize_mx(
-            out=w2_c[:].bitcast(FP8X4), scales=w2_s[:], in_=w2_b[:].rearrange("p t m j -> p (t m j)")
-        )
+        cast_w2_late(0)
+        quant_w2(0)
+        cast_w2_late(1)
+        quant_w2(1)
         normalise(3, 0, 0, CH)
         normalise(3, 0, CH, HALF)
-        normalise(3, 1, 0, HALF)
+        zt.append(sb.tile([P, PACK, HALF], BF16, name="zt1", tag="late", align_bytes=64))
+        for t in range(PACK):
+            normalise(t, 1, 0, HALF)
 
         def weave(copy, dst, src):
             copy(dst.rearrange("p (c i) t -> p c t i", i=4), src.rearrange("p t (c i) -> p c t i", i=4))
@@ -194,10 +207,13 @@ def tile_picked_inorm_none_po_kernel(
 
         def second(c):
             h = c // 2
-            for a in range(2):
-                acc = ps.tile([P, 2, CH], F32, name="y%d%d" % (c, a), tag="bank%d%d" % (2 * (c % 2) + a, h))
-                for e in range(2):
-                    t = 2 * a + e
+            last = c == 3
+            group = 1 if last else 2
+            for a in range(PACK // group):
+                bank = [(2, 1), (3, 1), (0, 0), (1, 0)][a] if last else (2 * (c % 2) + a, h)
+                acc = ps.tile([P, group, CH], F32, name="y%d%d" % (c, a), tag="bank%d%d" % bank)
+                for e in range(group):
+                    t = group * a + e
                     nc.tensor.matmul_mx(
                         out=acc[:, e, :],
                         lhsT=w2_c[:, t * P : (t + 1) * P].bitcast(FP8X4),
@@ -207,9 +223,8 @@ def tile_picked_inorm_none_po_kernel(
                         start=True,
                         stop=True,
                     )
-                nc.scalar.copy(y[h][:, 2 * a : 2 * a + 2, within(c)], acc[:])
-            if c % 2 == 1:
-                nc.sync.dma_start(out_rows[:, :, h * HALF : (h + 1) * HALF], y[h][:])
+                nc.scalar.copy(y[h][:, group * a : group * (a + 1), within(c)], acc[:])
+            nc.sync.dma_start(out_rows[:, :, c * CH : (c + 1) * CH], y[h][:, :, within(c)])
 
         def weave_y(c):
             weave(nc.vector.tensor_copy, y_b[c // 2][:, within(c), :], y[c // 2][:, :, within(c)])
@@ -227,20 +242,20 @@ def tile_picked_inorm_none_po_kernel(
                 nc.sync.dma_start(out_words[:, half], y_c[:, half].bitcast(I32))
 
         weave_z(nc.vector.tensor_copy, 0)
-        weave_z(nc.scalar.copy, 3)
         quant_z(0)
         weave_z(nc.vector.tensor_copy, 1)
         second(0)
         quant_z(1)
         weave_z(nc.vector.tensor_copy, 2)
         second(1)
+        weave_z(nc.vector.tensor_copy, 3)
         quant_z(2)
         quant_z(3)
         second(2)
-        second(3)
         weave_y(0)
         weave_y(1)
         planes(0, 2)
+        second(3)
         weave_y(2)
         planes(2, 3)
         weave_y(3)

@@ -47,17 +47,18 @@ def tile_picked_inorm_none_po_kernel(
         nc.vector.memset(warm[:, 0:1], 1.0)
         nc.scalar.activation(warm[:, 1:2], warm[:, 0:1], ACT.Abs_reciprocal_sqrt, bias=EPS)
 
-        nc.sync.dma_start(offsets[:], offs)
         nc.sync.dma_start(xw[:].bitcast(I32), x_words[0].rearrange("p c r -> p (c r)").bitcast(I32))
+        nc.sync.dma_start(offsets[:], offs)
         for q in range(4):
             nc.sync.dma_start(
                 xs[32 * q : 32 * q + 4, :].bitcast(I32), x_scales[0, 4 * q : 4 * q + 4, :].bitcast(I32)
             )
         nc.sync.dma_start(w1_raw[:], w1.rearrange("(p j) n -> p j n", j=PACK))
-        nc.sync.dma_start(gam[:], gamma.rearrange("(p t) o -> p (t o)", t=PACK))
         w2_rows = w2.rearrange("(p j) n -> p j n", j=PACK)
         for h in range(2):
             nc.sync.dma_start(w2_raw[h][:], w2_rows[:, :, h * (H // 2) : (h + 1) * (H // 2)])
+            if h == 0:
+                nc.sync.dma_start(gam[:], gamma.rearrange("(p t) o -> p (t o)", t=PACK))
 
         xg = tile("xg", [P, S], U32)
         xsg = tile("xsg", [P, S], U8)
@@ -79,8 +80,8 @@ def tile_picked_inorm_none_po_kernel(
                 in_=w1_b[t // 2][:, t % 2].rearrange("p m j -> p (m j)"),
             )
 
-        cast_w1(nc.vector.tensor_copy, 0, 0, 72)
-        cast_w1(nc.scalar.copy, 0, 72, P)
+        cast_w1(nc.vector.tensor_copy, 0, 0, 84)
+        cast_w1(nc.scalar.copy, 0, 84, P)
         cast_w1(nc.vector.tensor_copy, 1, 0, 40)
         cast_w1(nc.scalar.copy, 1, 80, P)
 
@@ -88,12 +89,11 @@ def tile_picked_inorm_none_po_kernel(
         early_stats = tile("early_stats", [P, 2, 12], F32)
         neg_gam = tile("neg_gam", [P, PACK], F32)
         mv = tile("mv", [P, PACK, 2], F32)
-        rstd = tile("rstd", [P, PACK], F32)
+        rstd = sb.tile([P, PACK], F32, name="rstd", tag="late2", align_bytes=64)
         coef = tile("coef", [P, PACK, 2], F32)
-        zt = [tile("zt0", [P, PACK, HALF], BF16)]
+        zt = [tile("zt%d" % c, [P, PACK, CH], BF16) for c in range(2)]
         w2_b = tile("w2_b", [P, PACK, P, PACK], BF16)
         w2_c = tile("w2_c", [P, H], U32)
-        w2_s = tile("w2_s", [P, H], U8)
 
         def cast_w2(copy, h, m0, m1):
             copy(
@@ -101,10 +101,14 @@ def tile_picked_inorm_none_po_kernel(
                 w2_raw[h][:].rearrange("p j (m t) -> p m j t", t=PACK)[:, m0:m1],
             )
 
-        def cast_w2_late(a):
-            nc.vector.tensor_copy(
-                w2_b[:].rearrange("p t m j -> p m j t")[:, 64:128, :, 2 * a : 2 * a + 2],
-                w2_raw[1][:].rearrange("p j (m t) -> p m j t", t=PACK)[:, :, :, 2 * a : 2 * a + 2],
+        def cast_w2_late():
+            nc.gpsimd.tensor_scalar(
+                w2_b[:].rearrange("p t m j -> p m t j")[:, 64:128],
+                w2_raw[1][:].rearrange("p j (m t) -> p m t j", t=PACK),
+                1.0,
+                0.0,
+                ALU.mult,
+                ALU.add,
             )
 
         def quant_w2(a):
@@ -115,9 +119,9 @@ def tile_picked_inorm_none_po_kernel(
                 in_=w2_b[:, 2 * a : 2 * a + 2].rearrange("p t m j -> p (t m j)"),
             )
 
-        stats = [early_stats[:, 0, :], early_stats[:, 1, :]] + [
-            w2_b[:, t].rearrange("p m j -> p (m j)").bitcast(F32)[:, 240:252] for t in (1, 3)
-        ]
+        last_stats = sb.tile([P, 12], F32, name="last_stats", tag="w2_scales", align_bytes=64)
+        first_stats = w2_b[:, 0].rearrange("p m j -> p (m j)").bitcast(F32)[:, 240:252]
+        stats = [first_stats, early_stats[:, 0, :], early_stats[:, 1, :], last_stats[:]]
 
         hb = [[None, None] for t in range(PACK)]
 
@@ -150,7 +154,7 @@ def tile_picked_inorm_none_po_kernel(
 
         def normalise(t, h, c0, c1):
             nc.scalar.activation(
-                zt[h][:, t, c0:c1], hb[t][h][:, c0:c1], ACT.Identity, bias=coef[:, t, 1:2], scale=coef[:, t, 0:1]
+                zt[2 * h + c0 // CH][:, t, :], hb[t][h][:, c0:c1], ACT.Identity, bias=coef[:, t, 1:2], scale=coef[:, t, 0:1]
             )
 
         quant_w1(0)
@@ -158,28 +162,38 @@ def tile_picked_inorm_none_po_kernel(
         cast_w1(nc.vector.tensor_copy, 1, 40, 80)
         quant_w1(2)
         quant_w1(3)
-        nc.scalar.activation(u[:, :, 0], gam[:], ACT.Copy)
-        nc.scalar.activation(neg_gam[:], gam[:], ACT.Copy, scale=-1.0)
         for t in range(PACK):
             project(t)
         cast_w2(nc.scalar.copy, 0, 0, 64)
+        nc.scalar.activation(u[:, :, 0], gam[:], ACT.Copy)
+        nc.scalar.activation(neg_gam[:], gam[:], ACT.Copy, scale=-1.0)
         for t in range(PACK):
             moments(t, 0)
             moments(t, 1)
             aggregate(t)
+            if t == 0:
+                cast_w2_late()
             inverse_deviation(t)
             if t > 0:
-                normalise(t - 1, 0, 0, HALF)
+                normalise(t - 1, 0, 0, CH)
             coefficients(t)
-        cast_w2_late(0)
+            if t > 0:
+                normalise(t - 1, 0, CH, HALF)
+        w2_s = sb.tile([P, H], U8, name="w2_s", tag="w2_scales", align_bytes=64)
         quant_w2(0)
-        cast_w2_late(1)
         quant_w2(1)
         normalise(3, 0, 0, CH)
         normalise(3, 0, CH, HALF)
-        zt.append(sb.tile([P, PACK, HALF], BF16, name="zt1", tag="late", align_bytes=64))
-        for t in range(PACK):
-            normalise(t, 1, 0, HALF)
+        zt.append(sb.tile([P, PACK, CH], BF16, name="zt2", tag="late", align_bytes=64))
+        zt.append(sb.tile([P, PACK, CH], BF16, name="zt3", tag="late2", align_bytes=64))
+        for t in range(2):
+            nc.vector.tensor_scalar(
+                zt[2][:, t, :], hb[t][1][:, 0:CH], coef[:, t, 0:1], coef[:, t, 1:2], ALU.mult, ALU.add
+            )
+        normalise(3, 1, 0, CH)
+        normalise(2, 1, 0, CH)
+        for t in (3, 2, 0, 1):
+            normalise(t, 1, CH, HALF)
 
         def weave(copy, dst, src):
             copy(dst.rearrange("p (c i) t -> p c t i", i=4), src.rearrange("p t (c i) -> p c t i", i=4))
@@ -187,18 +201,15 @@ def tile_picked_inorm_none_po_kernel(
         z_b = [tile("z_b%d" % c, [P, CH, PACK], BF16) for c in range(4)]
         z_c = [tile("z_c%d" % c, [P, CH], U32) for c in range(4)]
         z_s = [tile("z_s%d" % c, [P, CH], U8) for c in range(4)]
-        y = [tile("y%d" % h, [P, PACK, HALF], F32) for h in range(2)]
-        y_b = [tile("y_b%d" % h, [P, HALF, PACK], BF16) for h in range(2)]
+        y = [tile("y%d" % c, [P, PACK, CH], F32) for c in range(4)]
+        y_b = [tile("y_b%d" % c, [P, CH, PACK], BF16) for c in range(4)]
         y_c = tile("y_c", [P, S], U32)
         y_s = tile("y_s", [P, S], U8)
         out_rows = out_0.rearrange("(p t) n -> p t n", t=PACK)
         out_words = out_1[0].rearrange("p c r -> p (c r)").bitcast(I32)
 
-        def within(c):
-            return slice((c % 2) * CH, (c % 2 + 1) * CH)
-
         def weave_z(copy, c):
-            weave(copy, z_b[c][:], zt[c // 2][:, :, within(c)])
+            weave(copy, z_b[c][:], zt[c][:])
 
         def quant_z(c):
             nc.vector.quantize_mx(
@@ -223,22 +234,19 @@ def tile_picked_inorm_none_po_kernel(
                         start=True,
                         stop=True,
                     )
-                nc.scalar.copy(y[h][:, group * a : group * (a + 1), within(c)], acc[:])
-            nc.sync.dma_start(out_rows[:, :, c * CH : (c + 1) * CH], y[h][:, :, within(c)])
+                nc.scalar.copy(y[c][:, group * a : group * (a + 1), :], acc[:])
+            nc.sync.dma_start(out_rows[:, :, c * CH : (c + 1) * CH], y[c][:])
 
         def weave_y(c):
-            weave(nc.vector.tensor_copy, y_b[c // 2][:, within(c), :], y[c // 2][:, :, within(c)])
+            weave(nc.vector.tensor_copy, y_b[c][:], y[c][:])
 
-        def planes(c0, c1):
-            cols = slice(c0 * CH, c1 * CH)
-            h = c0 // 2
+        def planes(c):
+            cols = slice(c * CH, (c + 1) * CH)
             nc.vector.quantize_mx(
-                out=y_c[:, cols].bitcast(FP8X4),
-                scales=y_s[:, cols],
-                in_=y_b[h][:, c0 * CH - h * HALF : c1 * CH - h * HALF, :].rearrange("p n t -> p (n t)"),
+                out=y_c[:, cols].bitcast(FP8X4), scales=y_s[:, cols], in_=y_b[c][:].rearrange("p n t -> p (n t)")
             )
-            if c1 % 2 == 0:
-                half = slice(h * HALF, (h + 1) * HALF)
+            if c % 2 == 1:
+                half = slice((c - 1) * CH, (c + 1) * CH)
                 nc.sync.dma_start(out_words[:, half], y_c[:, half].bitcast(I32))
 
         weave_z(nc.vector.tensor_copy, 0)
@@ -248,18 +256,16 @@ def tile_picked_inorm_none_po_kernel(
         quant_z(1)
         weave_z(nc.vector.tensor_copy, 2)
         second(1)
-        weave_z(nc.vector.tensor_copy, 3)
         quant_z(2)
+        weave_z(nc.scalar.copy, 3)
         quant_z(3)
         second(2)
-        weave_y(0)
-        weave_y(1)
-        planes(0, 2)
         second(3)
-        weave_y(2)
-        planes(2, 3)
-        weave_y(3)
-        planes(3, 4)
+        for c in range(4):
+            weave_y(c)
+            if c > 0:
+                planes(c - 1)
+        planes(3)
         for q in range(4):
             queue = nc.sync if q < 2 else nc.scalar
             queue.dma_start(

@@ -32,17 +32,20 @@ def tile_picked_inorm_none_po_kernel(
         sb = ctx.enter_context(tc.tile_pool(name="sb", bufs=1))
         ps = ctx.enter_context(tc.psum_pool(name="ps", bufs=1))
 
-        def tile(name, shape, dtype):
-            return sb.tile(shape, dtype, name=name, align_bytes=64)
+        def tile(name, shape, dtype, tag=None):
+            return sb.tile(shape, dtype, name=name, tag=tag or name, align_bytes=64)
 
         offsets = sb.tile([P, S // 16], U16, name="offsets")
         xw = tile("xw", [P, T], U32)
         xs = tile("xs", [P, T], U8)
-        w1_raw = tile("w1_raw", [P, PACK, H], F32)
-        w2_raw = [tile("w2_raw%d" % h, [P, PACK, H // 2], F32) for h in range(2)]
-        gam = tile("gam", [P, PACK], F32)
+        w1_cuts = [0, 256, 512]
+        w2_cuts = [0, 256, 384, 512]
+        w1_raw = [tile("w1_raw%d" % h, [P, PACK, w1_cuts[h + 1] - w1_cuts[h]], F32) for h in range(2)]
+        w2_raw = [tile("w2_raw%d" % h, [P, PACK, w2_cuts[h + 1] - w2_cuts[h]], F32) for h in range(3)]
+        gam = tile("gam", [P, 2, PACK], F32)
         warm = tile("warm", [P, 2], F32)
 
+        nc.gpsimd.dma_start(gam[:, 0, :], gamma.rearrange("(p t) o -> p (t o)", t=PACK))
         nc.vector.memset(xs[:].bitcast(I32), 0)
         nc.vector.memset(warm[:, 0:1], 1.0)
         nc.scalar.activation(warm[:, 1:2], warm[:, 0:1], ACT.Abs_reciprocal_sqrt, bias=EPS)
@@ -53,62 +56,56 @@ def tile_picked_inorm_none_po_kernel(
             nc.sync.dma_start(
                 xs[32 * q : 32 * q + 4, :].bitcast(I32), x_scales[0, 4 * q : 4 * q + 4, :].bitcast(I32)
             )
-        nc.sync.dma_start(w1_raw[:], w1.rearrange("(p j) n -> p j n", j=PACK))
+        w1_rows = w1.rearrange("(p j) n -> p j n", j=PACK)
         w2_rows = w2.rearrange("(p j) n -> p j n", j=PACK)
         for h in range(2):
-            nc.sync.dma_start(w2_raw[h][:], w2_rows[:, :, h * (H // 2) : (h + 1) * (H // 2)])
-            if h == 0:
-                nc.sync.dma_start(gam[:], gamma.rearrange("(p t) o -> p (t o)", t=PACK))
+            nc.sync.dma_start(w1_raw[h][:], w1_rows[:, :, w1_cuts[h] : w1_cuts[h + 1]])
+        for h in range(3):
+            nc.sync.dma_start(w2_raw[h][:], w2_rows[:, :, w2_cuts[h] : w2_cuts[h + 1]])
 
         xg = tile("xg", [P, S], U32)
         xsg = tile("xsg", [P, S], U8)
         nc.vector.tensor_copy(xg[:], xw[:].indirect(offsets[:]))
         nc.vector.tensor_copy(xsg[:], xs[:].indirect(offsets[:]))
 
-        w1_src = w1_raw[:].rearrange("p j (m t) -> p m j t", t=PACK)
-        w1_b = [tile("w1_b%d" % a, [P, 2, P, PACK], BF16) for a in range(2)]
+        w1_b = tile("w1_b", [P, PACK, P, PACK], BF16, tag="w_b")
         w1_c = [tile("w1_c%d" % t, [P, P], U32) for t in range(PACK)]
         w1_s = [tile("w1_s%d" % t, [P, P], U8) for t in range(PACK)]
 
-        def cast_w1(copy, a, m0, m1):
-            copy(w1_b[a][:].rearrange("p t m j -> p m j t")[:, m0:m1], w1_src[:, m0:m1, :, 2 * a : 2 * a + 2])
+        def cast_w1(copy, h, m0, m1, t0, t1):
+            base = w1_cuts[h] // PACK
+            copy(
+                w1_b[:].rearrange("p t m j -> p m j t")[:, base + m0 : base + m1, :, t0:t1],
+                w1_raw[h][:].rearrange("p j (m t) -> p m j t", t=PACK)[:, m0:m1, :, t0:t1],
+            )
 
         def quant_w1(t):
             nc.vector.quantize_mx(
-                out=w1_c[t][:].bitcast(FP8X4),
-                scales=w1_s[t][:],
-                in_=w1_b[t // 2][:, t % 2].rearrange("p m j -> p (m j)"),
+                out=w1_c[t][:].bitcast(FP8X4), scales=w1_s[t][:], in_=w1_b[:, t].rearrange("p m j -> p (m j)")
             )
 
-        cast_w1(nc.vector.tensor_copy, 0, 0, 84)
-        cast_w1(nc.scalar.copy, 0, 84, P)
-        cast_w1(nc.vector.tensor_copy, 1, 0, 40)
-        cast_w1(nc.scalar.copy, 1, 80, P)
+        cast_w1(nc.scalar.copy, 0, 0, 64, 0, 4)
+        cast_w1(nc.vector.tensor_copy, 1, 0, 64, 0, 2)
+        cast_w1(nc.vector.tensor_copy, 1, 0, 20, 2, 4)
+        cast_w1(nc.scalar.copy, 1, 20, 64, 2, 4)
+        for t in range(PACK):
+            quant_w1(t)
 
-        u = sb.tile([P, PACK, 2], F32, name="u", tag="late", align_bytes=64)
-        early_stats = tile("early_stats", [P, 2, 12], F32)
-        neg_gam = tile("neg_gam", [P, PACK], F32)
+        stats = tile("stats", [P, PACK, 12], F32)
+        neg_gam = tile("neg_gam", [P, PACK], F32, tag="late")
         mv = tile("mv", [P, PACK, 2], F32)
-        rstd = sb.tile([P, PACK], F32, name="rstd", tag="late2", align_bytes=64)
+        rstd = tile("rstd", [P, PACK], F32, tag="late2")
         coef = tile("coef", [P, PACK, 2], F32)
         zt = [tile("zt%d" % c, [P, PACK, CH], BF16) for c in range(2)]
-        w2_b = tile("w2_b", [P, PACK, P, PACK], BF16)
+        w2_b = tile("w2_b", [P, PACK, P, PACK], BF16, tag="w_b")
         w2_c = tile("w2_c", [P, H], U32)
+        w2_s = tile("w2_s", [P, H], U8)
 
-        def cast_w2(copy, h, m0, m1):
-            copy(
-                w2_b[:].rearrange("p t m j -> p m j t")[:, h * 64 + m0 : h * 64 + m1],
-                w2_raw[h][:].rearrange("p j (m t) -> p m j t", t=PACK)[:, m0:m1],
-            )
-
-        def cast_w2_late():
-            nc.gpsimd.tensor_scalar(
-                w2_b[:].rearrange("p t m j -> p m t j")[:, 64:128],
-                w2_raw[1][:].rearrange("p j (m t) -> p m t j", t=PACK),
-                1.0,
-                0.0,
-                ALU.mult,
-                ALU.add,
+        def w2_views(h, order):
+            m0, m1 = w2_cuts[h] // PACK, w2_cuts[h + 1] // PACK
+            return (
+                w2_b[:].rearrange("p t m j -> " + order)[:, m0:m1],
+                w2_raw[h][:].rearrange("p j (m t) -> " + order, t=PACK),
             )
 
         def quant_w2(a):
@@ -119,16 +116,14 @@ def tile_picked_inorm_none_po_kernel(
                 in_=w2_b[:, 2 * a : 2 * a + 2].rearrange("p t m j -> p (t m j)"),
             )
 
-        last_stats = sb.tile([P, 12], F32, name="last_stats", tag="w2_scales", align_bytes=64)
-        first_stats = w2_b[:, 0].rearrange("p m j -> p (m j)").bitcast(F32)[:, 240:252]
-        stats = [first_stats, early_stats[:, 0, :], early_stats[:, 1, :], last_stats[:]]
-
-        hb = [[None, None] for t in range(PACK)]
+        widths = [HALF] * PACK
+        banks = [[2 * t, 2 * t + 1] for t in range(PACK)]
+        hb = [[] for t in range(PACK)]
 
         def project(t):
-            for h in range(2):
-                cols = slice(h * HALF, (h + 1) * HALF)
-                hb[t][h] = ps.tile([P, HALF], F32, name="h%d%d" % (t, h), tag="bank%d%d" % (t, h))
+            for h, bank in enumerate(banks[t]):
+                cols = slice(h * widths[t], (h + 1) * widths[t])
+                hb[t].append(ps.tile([P, widths[t]], F32, name="h%d%d" % (t, h), tag="bank%d" % bank))
                 nc.tensor.matmul_mx(
                     out=hb[t][h][:],
                     lhsT=w1_c[t][:].bitcast(FP8X4),
@@ -139,64 +134,56 @@ def tile_picked_inorm_none_po_kernel(
                     stop=True,
                 )
 
-        def moments(t, h):
-            nc.vector.bn_stats(stats[t][:, 6 * h : 6 * h + 6], hb[t][h][:])
+        def h_chunk(t, c):
+            h, c0 = divmod(c * CH, widths[t])
+            return hb[t][h][:, c0 : c0 + CH]
+
+        def moments(t):
+            for h in range(len(banks[t])):
+                nc.vector.bn_stats(stats[:, t, 6 * h : 6 * h + 6], hb[t][h][:])
 
         def aggregate(t):
-            nc.vector.bn_aggr(mv[:, t, :], stats[t])
+            nc.vector.bn_aggr(mv[:, t, :], stats[:, t, 0 : 6 * len(banks[t])])
 
         def inverse_deviation(t):
             nc.scalar.activation(rstd[:, t : t + 1], mv[:, t, 1:2], ACT.Abs_reciprocal_sqrt, bias=EPS)
-            nc.scalar.activation(u[:, t, 1:2], mv[:, t, 0:1], ACT.Copy, scale=neg_gam[:, t : t + 1])
+            nc.scalar.activation(gam[:, 1, t : t + 1], mv[:, t, 0:1], ACT.Copy, scale=neg_gam[:, t : t + 1])
 
         def coefficients(t):
-            nc.scalar.activation(coef[:, t, :], u[:, t, :], ACT.Copy, scale=rstd[:, t : t + 1])
+            nc.scalar.activation(coef[:, t, :], gam[:, :, t], ACT.Copy, scale=rstd[:, t : t + 1])
 
-        def normalise(t, h, c0, c1):
+        def normalise(t, c):
             nc.scalar.activation(
-                zt[2 * h + c0 // CH][:, t, :], hb[t][h][:, c0:c1], ACT.Identity, bias=coef[:, t, 1:2], scale=coef[:, t, 0:1]
+                zt[c][:, t, :], h_chunk(t, c), ACT.Identity, bias=coef[:, t, 1:2], scale=coef[:, t, 0:1]
             )
 
-        quant_w1(0)
-        quant_w1(1)
-        cast_w1(nc.vector.tensor_copy, 1, 40, 80)
-        quant_w1(2)
-        quant_w1(3)
+        def normalise_on_vector(t, c):
+            nc.vector.tensor_scalar(zt[c][:, t, :], h_chunk(t, c), coef[:, t, 0:1], coef[:, t, 1:2], ALU.mult, ALU.add)
+
         for t in range(PACK):
             project(t)
-        cast_w2(nc.scalar.copy, 0, 0, 64)
-        nc.scalar.activation(u[:, :, 0], gam[:], ACT.Copy)
-        nc.scalar.activation(neg_gam[:], gam[:], ACT.Copy, scale=-1.0)
+        nc.scalar.copy(*w2_views(0, "p m j t"))
+        nc.gpsimd.tensor_scalar(neg_gam[:], gam[:, 0, :], -1.0, 0.0, ALU.mult, ALU.add)
+        for h in (1, 2):
+            nc.gpsimd.tensor_scalar(*w2_views(h, "p m t j"), 1.0, 0.0, ALU.mult, ALU.add)
         for t in range(PACK):
-            moments(t, 0)
-            moments(t, 1)
+            moments(t)
+            if t == 3:
+                quant_w2(0)
             aggregate(t)
-            if t == 0:
-                cast_w2_late()
             inverse_deviation(t)
             if t > 0:
-                normalise(t - 1, 0, 0, CH)
+                normalise(t - 1, 0)
             coefficients(t)
             if t > 0:
-                normalise(t - 1, 0, CH, HALF)
-        w2_s = sb.tile([P, H], U8, name="w2_s", tag="w2_scales", align_bytes=64)
-        quant_w2(0)
+                normalise(t - 1, 1)
         quant_w2(1)
-        normalise(3, 0, 0, CH)
-        normalise(3, 0, CH, HALF)
-        zt.append(sb.tile([P, PACK, CH], BF16, name="zt2", tag="late", align_bytes=64))
-        zt.append(sb.tile([P, PACK, CH], BF16, name="zt3", tag="late2", align_bytes=64))
-        for t in range(2):
-            nc.vector.tensor_scalar(
-                zt[2][:, t, :], hb[t][1][:, 0:CH], coef[:, t, 0:1], coef[:, t, 1:2], ALU.mult, ALU.add
-            )
-        normalise(3, 1, 0, CH)
-        normalise(2, 1, 0, CH)
-        for t in (3, 2, 0, 1):
-            normalise(t, 1, CH, HALF)
 
-        def weave(copy, dst, src):
-            copy(dst.rearrange("p (c i) t -> p c t i", i=4), src.rearrange("p t (c i) -> p c t i", i=4))
+        def weave(copy, dst, src, t1=PACK):
+            copy(
+                dst.rearrange("p (c i) t -> p c t i", i=4)[:, :, 0:t1],
+                src.rearrange("p t (c i) -> p c t i", i=4)[:, :, 0:t1],
+            )
 
         z_b = [tile("z_b%d" % c, [P, CH, PACK], BF16) for c in range(4)]
         z_c = [tile("z_c%d" % c, [P, CH], U32) for c in range(4)]
@@ -205,28 +192,26 @@ def tile_picked_inorm_none_po_kernel(
         y_b = [tile("y_b%d" % c, [P, CH, PACK], BF16) for c in range(4)]
         y_c = tile("y_c", [P, S], U32)
         y_s = tile("y_s", [P, S], U8)
+        centred = tile("centred", [P, CH], F32)
         out_rows = out_0.rearrange("(p t) n -> p t n", t=PACK)
         out_words = out_1[0].rearrange("p c r -> p (c r)").bitcast(I32)
-
-        def weave_z(copy, c):
-            weave(copy, z_b[c][:], zt[c][:])
 
         def quant_z(c):
             nc.vector.quantize_mx(
                 out=z_c[c][:].bitcast(FP8X4), scales=z_s[c][:], in_=z_b[c][:].rearrange("p n t -> p (n t)")
             )
 
+        y_banks = [[0, 2], [4, 6], [1, 3], [5, 7, 0, 2]]
+        acc = [[] for c in range(4)]
+
         def second(c):
-            h = c // 2
-            last = c == 3
-            group = 1 if last else 2
-            for a in range(PACK // group):
-                bank = [(2, 1), (3, 1), (0, 0), (1, 0)][a] if last else (2 * (c % 2) + a, h)
-                acc = ps.tile([P, group, CH], F32, name="y%d%d" % (c, a), tag="bank%d%d" % bank)
+            group = PACK // len(y_banks[c])
+            for a, bank in enumerate(y_banks[c]):
+                acc[c].append(ps.tile([P, group, CH], F32, name="y%d%d" % (c, a), tag="bank%d" % bank))
                 for e in range(group):
                     t = group * a + e
                     nc.tensor.matmul_mx(
-                        out=acc[:, e, :],
+                        out=acc[c][a][:, e, :],
                         lhsT=w2_c[:, t * P : (t + 1) * P].bitcast(FP8X4),
                         lhsT_scale=w2_s[:, t * P : (t + 1) * P],
                         rhs=z_c[c][:].bitcast(FP8X4),
@@ -234,11 +219,13 @@ def tile_picked_inorm_none_po_kernel(
                         start=True,
                         stop=True,
                     )
-                nc.scalar.copy(y[c][:, group * a : group * (a + 1), :], acc[:])
-            nc.sync.dma_start(out_rows[:, :, c * CH : (c + 1) * CH], y[c][:])
 
-        def weave_y(c):
-            weave(nc.vector.tensor_copy, y_b[c][:], y[c][:])
+        def drain(copy, c, a):
+            group = PACK // len(y_banks[c])
+            copy(y[c][:, group * a : group * (a + 1), :], acc[c][a][:])
+
+        def store(c):
+            nc.sync.dma_start(out_rows[:, :, c * CH : (c + 1) * CH], y[c][:])
 
         def planes(c):
             cols = slice(c * CH, (c + 1) * CH)
@@ -249,20 +236,38 @@ def tile_picked_inorm_none_po_kernel(
                 half = slice((c - 1) * CH, (c + 1) * CH)
                 nc.sync.dma_start(out_words[:, half], y_c[:, half].bitcast(I32))
 
-        weave_z(nc.vector.tensor_copy, 0)
+        nc.vector.tensor_scalar(centred[:], h_chunk(3, 0), mv[:, 3, 0:1], gam[:, 0, 3:4], ALU.subtract, ALU.mult)
+        nc.vector.tensor_scalar(z_b[0][:, :, 3], centred[:], rstd[:, 3:4], None, ALU.mult)
+        weave(nc.vector.tensor_copy, z_b[0][:], zt[0][:], 3)
+        normalise(3, 1)
+        zt.append(tile("zt2", [P, PACK, CH], BF16, tag="late"))
+        zt.append(tile("zt3", [P, PACK, CH], BF16, tag="late2"))
+        normalise(3, 2)
+        normalise(2, 2)
+        normalise_on_vector(0, 2)
         quant_z(0)
-        weave_z(nc.vector.tensor_copy, 1)
+        weave(nc.vector.tensor_copy, z_b[1][:], zt[1][:])
+        normalise_on_vector(1, 2)
+        for t in (3, 2, 0, 1):
+            normalise(t, 3)
         second(0)
         quant_z(1)
-        weave_z(nc.vector.tensor_copy, 2)
+        weave(nc.vector.tensor_copy, z_b[2][:], zt[2][:])
         second(1)
+        weave(nc.scalar.copy, z_b[3][:], zt[3][:])
         quant_z(2)
-        weave_z(nc.scalar.copy, 3)
         quant_z(3)
+        drain(nc.scalar.copy, 0, 0)
+        drain(nc.vector.tensor_copy, 0, 1)
+        store(0)
         second(2)
         second(3)
+        for c in range(1, 4):
+            for a in range(len(y_banks[c])):
+                drain(nc.scalar.copy, c, a)
+            store(c)
         for c in range(4):
-            weave_y(c)
+            weave(nc.vector.tensor_copy, y_b[c][:], y[c][:])
             if c > 0:
                 planes(c - 1)
         planes(3)

@@ -38,14 +38,13 @@ def tile_picked_inorm_none_po_kernel(
         offsets = sb.tile([P, S // 16], U16, name="offsets")
         xw = tile("xw", [P, T], U32)
         xs = tile("xs", [P, T], U8)
-        w1_cuts = [0, 256, 512]
         w2_cuts = [0, 256, 384, 512]
-        w1_raw = [tile("w1_raw%d" % h, [P, PACK, w1_cuts[h + 1] - w1_cuts[h]], F32) for h in range(2)]
+        w1_raw = tile("w1_raw", [P, PACK, H], F32)
         w2_raw = [tile("w2_raw%d" % h, [P, PACK, w2_cuts[h + 1] - w2_cuts[h]], F32) for h in range(3)]
         gam = tile("gam", [P, 2, PACK], F32)
         warm = tile("warm", [P, 2], F32)
 
-        nc.gpsimd.dma_start(gam[:, 0, :], gamma.rearrange("(p t) o -> p (t o)", t=PACK))
+        nc.scalar.dma_start(gam[:, 0, :], gamma.rearrange("(p t) o -> p (t o)", t=PACK))
         nc.vector.memset(xs[:].bitcast(I32), 0)
         nc.vector.memset(warm[:, 0:1], 1.0)
         nc.scalar.activation(warm[:, 1:2], warm[:, 0:1], ACT.Abs_reciprocal_sqrt, bias=EPS)
@@ -56,10 +55,8 @@ def tile_picked_inorm_none_po_kernel(
             nc.sync.dma_start(
                 xs[32 * q : 32 * q + 4, :].bitcast(I32), x_scales[0, 4 * q : 4 * q + 4, :].bitcast(I32)
             )
-        w1_rows = w1.rearrange("(p j) n -> p j n", j=PACK)
         w2_rows = w2.rearrange("(p j) n -> p j n", j=PACK)
-        for h in range(2):
-            nc.sync.dma_start(w1_raw[h][:], w1_rows[:, :, w1_cuts[h] : w1_cuts[h + 1]])
+        nc.sync.dma_start(w1_raw[:], w1.rearrange("(p j) n -> p j n", j=PACK))
         for h in range(3):
             nc.sync.dma_start(w2_raw[h][:], w2_rows[:, :, w2_cuts[h] : w2_cuts[h + 1]])
 
@@ -72,11 +69,10 @@ def tile_picked_inorm_none_po_kernel(
         w1_c = [tile("w1_c%d" % t, [P, P], U32) for t in range(PACK)]
         w1_s = [tile("w1_s%d" % t, [P, P], U8) for t in range(PACK)]
 
-        def cast_w1(copy, h, m0, m1, t0, t1):
-            base = w1_cuts[h] // PACK
+        def cast_w1(copy, a, m0, m1):
             copy(
-                w1_b[:].rearrange("p t m j -> p m j t")[:, base + m0 : base + m1, :, t0:t1],
-                w1_raw[h][:].rearrange("p j (m t) -> p m j t", t=PACK)[:, m0:m1, :, t0:t1],
+                w1_b[:].rearrange("p t m j -> p m j t")[:, m0:m1, :, 2 * a : 2 * a + 2],
+                w1_raw[:].rearrange("p j (m t) -> p m j t", t=PACK)[:, m0:m1, :, 2 * a : 2 * a + 2],
             )
 
         def quant_w1(t):
@@ -84,12 +80,15 @@ def tile_picked_inorm_none_po_kernel(
                 out=w1_c[t][:].bitcast(FP8X4), scales=w1_s[t][:], in_=w1_b[:, t].rearrange("p m j -> p (m j)")
             )
 
-        cast_w1(nc.scalar.copy, 0, 0, 64, 0, 4)
-        cast_w1(nc.vector.tensor_copy, 1, 0, 64, 0, 2)
-        cast_w1(nc.vector.tensor_copy, 1, 0, 20, 2, 4)
-        cast_w1(nc.scalar.copy, 1, 20, 64, 2, 4)
-        for t in range(PACK):
-            quant_w1(t)
+        cast_w1(nc.vector.tensor_copy, 0, 0, 84)
+        cast_w1(nc.scalar.copy, 0, 84, P)
+        cast_w1(nc.vector.tensor_copy, 1, 0, 40)
+        cast_w1(nc.scalar.copy, 1, 80, P)
+        quant_w1(0)
+        quant_w1(1)
+        cast_w1(nc.vector.tensor_copy, 1, 40, 80)
+        quant_w1(2)
+        quant_w1(3)
 
         stats = tile("stats", [P, PACK, 12], F32)
         neg_gam = tile("neg_gam", [P, PACK], F32, tag="late")
@@ -156,9 +155,6 @@ def tile_picked_inorm_none_po_kernel(
             nc.scalar.activation(
                 zt[c][:, t, :], h_chunk(t, c), ACT.Identity, bias=coef[:, t, 1:2], scale=coef[:, t, 0:1]
             )
-
-        def normalise_on_vector(t, c):
-            nc.vector.tensor_scalar(zt[c][:, t, :], h_chunk(t, c), coef[:, t, 0:1], coef[:, t, 1:2], ALU.mult, ALU.add)
 
         for t in range(PACK):
             project(t)
@@ -242,25 +238,21 @@ def tile_picked_inorm_none_po_kernel(
         normalise(3, 1)
         zt.append(tile("zt2", [P, PACK, CH], BF16, tag="late"))
         zt.append(tile("zt3", [P, PACK, CH], BF16, tag="late2"))
-        normalise(3, 2)
-        normalise(2, 2)
-        normalise_on_vector(0, 2)
+        for c in (2, 3):
+            for t in (3, 2, 0, 1):
+                normalise(t, c)
         quant_z(0)
         weave(nc.vector.tensor_copy, z_b[1][:], zt[1][:])
-        normalise_on_vector(1, 2)
-        for t in (3, 2, 0, 1):
-            normalise(t, 3)
-        second(0)
-        quant_z(1)
         weave(nc.vector.tensor_copy, z_b[2][:], zt[2][:])
-        second(1)
-        weave(nc.scalar.copy, z_b[3][:], zt[3][:])
+        quant_z(1)
         quant_z(2)
+        weave(nc.vector.tensor_copy, z_b[3][:], zt[3][:])
         quant_z(3)
-        drain(nc.scalar.copy, 0, 0)
-        drain(nc.vector.tensor_copy, 0, 1)
+        for c in range(3):
+            second(c)
+        for a in range(2):
+            drain(nc.scalar.copy, 0, a)
         store(0)
-        second(2)
         second(3)
         for c in range(1, 4):
             for a in range(len(y_banks[c])):

@@ -40,11 +40,12 @@ def tile_picked_inorm_none_po_kernel(
         xs = tile("xs", [P, T], U8)
         w2_cuts = [0, 256, 384, 512]
         w1_raw = tile("w1_raw", [P, PACK, H], F32)
-        w2_raw = [tile("w2_raw%d" % h, [P, PACK, w2_cuts[h + 1] - w2_cuts[h]], F32) for h in range(3)]
-        gam = tile("gam", [P, 2, PACK], F32)
+        w2_raw = [
+            tile("w2_raw%d" % h, [P, PACK, w2_cuts[h + 1] - w2_cuts[h]], F32, tag="late" if h == 0 else None)
+            for h in range(3)
+        ]
         warm = tile("warm", [P, 2], F32)
 
-        nc.scalar.dma_start(gam[:, 0, :], gamma.rearrange("(p t) o -> p (t o)", t=PACK))
         nc.vector.memset(xs[:].bitcast(I32), 0)
         nc.vector.memset(warm[:, 0:1], 1.0)
         nc.scalar.activation(warm[:, 1:2], warm[:, 0:1], ACT.Abs_reciprocal_sqrt, bias=EPS)
@@ -64,6 +65,8 @@ def tile_picked_inorm_none_po_kernel(
         xsg = tile("xsg", [P, S], U8)
         nc.vector.tensor_copy(xg[:], xw[:].indirect(offsets[:]))
         nc.vector.tensor_copy(xsg[:], xs[:].indirect(offsets[:]))
+        gam = tile("gam", [P, 2, PACK], F32, tag="xw")
+        nc.scalar.dma_start(gam[:, 0, :], gamma.rearrange("(p t) o -> p (t o)", t=PACK))
 
         w1_b = tile("w1_b", [P, PACK, P, PACK], BF16, tag="w_b")
         w1_c = [tile("w1_c%d" % t, [P, P], U32) for t in range(PACK)]
@@ -91,7 +94,6 @@ def tile_picked_inorm_none_po_kernel(
         quant_w1(3)
 
         stats = tile("stats", [P, PACK, 12], F32)
-        neg_gam = tile("neg_gam", [P, PACK], F32, tag="late")
         mv = tile("mv", [P, PACK, 2], F32)
         rstd = tile("rstd", [P, PACK], F32, tag="late2")
         coef = tile("coef", [P, PACK, 2], F32)
@@ -107,13 +109,14 @@ def tile_picked_inorm_none_po_kernel(
                 w2_raw[h][:].rearrange("p j (m t) -> " + order, t=PACK),
             )
 
-        def quant_w2(a):
-            cols = slice(2 * a * P, 2 * (a + 1) * P)
-            nc.vector.quantize_mx(
-                out=w2_c[:, cols].bitcast(FP8X4),
-                scales=w2_s[:, cols],
-                in_=w2_b[:, 2 * a : 2 * a + 2].rearrange("p t m j -> p (t m j)"),
-            )
+        def quant_w2(h):
+            for t in range(PACK):
+                cols = slice(t * P + 64 * h, t * P + 64 * (h + 1))
+                nc.vector.quantize_mx(
+                    out=w2_c[:, cols].bitcast(FP8X4),
+                    scales=w2_s[:, cols],
+                    in_=w2_b[:, t, 64 * h : 64 * (h + 1)].rearrange("p m j -> p (m j)"),
+                )
 
         widths = [HALF] * PACK
         banks = [[2 * t, 2 * t + 1] for t in range(PACK)]
@@ -159,13 +162,12 @@ def tile_picked_inorm_none_po_kernel(
         for t in range(PACK):
             project(t)
         nc.scalar.copy(*w2_views(0, "p m j t"))
-        nc.gpsimd.tensor_scalar(neg_gam[:], gam[:, 0, :], -1.0, 0.0, ALU.mult, ALU.add)
+        neg_gam = tile("neg_gam", [P, PACK], F32, tag="late")
+        nc.scalar.activation(neg_gam[:], gam[:, 0, :], ACT.Copy, scale=-1.0)
         for h in (1, 2):
             nc.gpsimd.tensor_scalar(*w2_views(h, "p m t j"), 1.0, 0.0, ALU.mult, ALU.add)
         for t in range(PACK):
             moments(t)
-            if t == 3:
-                quant_w2(0)
             aggregate(t)
             inverse_deviation(t)
             if t > 0:
@@ -173,7 +175,6 @@ def tile_picked_inorm_none_po_kernel(
             coefficients(t)
             if t > 0:
                 normalise(t - 1, 1)
-        quant_w2(1)
 
         def weave(copy, dst, src, t1=PACK):
             copy(
@@ -235,6 +236,8 @@ def tile_picked_inorm_none_po_kernel(
         nc.vector.tensor_scalar(centred[:], h_chunk(3, 0), mv[:, 3, 0:1], gam[:, 0, 3:4], ALU.subtract, ALU.mult)
         nc.vector.tensor_scalar(z_b[0][:, :, 3], centred[:], rstd[:, 3:4], None, ALU.mult)
         weave(nc.vector.tensor_copy, z_b[0][:], zt[0][:], 3)
+        quant_w2(0)
+        quant_w2(1)
         normalise(3, 1)
         zt.append(tile("zt2", [P, PACK, CH], BF16, tag="late"))
         zt.append(tile("zt3", [P, PACK, CH], BF16, tag="late2"))

@@ -231,7 +231,8 @@ def tile_picked_inorm_none_po_kernel(
             )
             if c % 2 == 1:
                 half = slice((c - 1) * CH, (c + 1) * CH)
-                nc.sync.dma_start(out_words[:, half], y_c[:, half].bitcast(I32))
+                queue = nc.sync if c == 1 else nc.scalar
+                queue.dma_start(out_words[:, half], y_c[:, half].bitcast(I32))
 
         nc.vector.tensor_scalar(centred[:], h_chunk(3, 0), mv[:, 3, 0:1], gam[:, 0, 3:4], ALU.subtract, ALU.mult)
         nc.vector.tensor_scalar(z_b[0][:, :, 3], centred[:], rstd[:, 3:4], None, ALU.mult)
@@ -267,7 +268,7 @@ def tile_picked_inorm_none_po_kernel(
                 planes(c - 1)
         planes(3)
         for q in range(4):
-            queue = nc.sync if q < 2 else nc.scalar
+            queue = nc.sync if q < 3 else nc.scalar
             queue.dma_start(
                 out_2[0, 4 * q : 4 * q + 4, :].bitcast(I32), y_s[32 * q : 32 * q + 4, :].bitcast(I32)
             )

@@ -185,7 +185,8 @@ def tile_picked_inorm_none_po_kernel(
         z_b = [tile("z_b%d" % c, [P, CH, PACK], BF16) for c in range(4)]
         z_c = [tile("z_c%d" % c, [P, CH], U32) for c in range(4)]
         z_s = [tile("z_s%d" % c, [P, CH], U8) for c in range(4)]
-        y = [tile("y%d" % c, [P, PACK, CH], F32) for c in range(4)]
+        y_half = [tile("y%d" % h, [P, PACK, HALF], F32) for h in range(2)]
+        y = [y_half[c // 2][:, :, (c % 2) * CH : (c % 2 + 1) * CH] for c in range(4)]
         y_b = [tile("y_b%d" % c, [P, CH, PACK], BF16) for c in range(4)]
         y_c = tile("y_c", [P, S], U32)
         y_s = tile("y_s", [P, S], U8)
@@ -221,8 +222,10 @@ def tile_picked_inorm_none_po_kernel(
             group = PACK // len(y_banks[c])
             copy(y[c][:, group * a : group * (a + 1), :], acc[c][a][:])
 
-        def store(c):
-            nc.sync.dma_start(out_rows[:, :, c * CH : (c + 1) * CH], y[c][:])
+        def store(h, u):
+            nc.sync.dma_start(
+                out_rows[:, 2 * u : 2 * u + 2, h * HALF : (h + 1) * HALF], y_half[h][:, 2 * u : 2 * u + 2, :]
+            )
 
         def planes(c):
             cols = slice(c * CH, (c + 1) * CH)
@@ -256,14 +259,15 @@ def tile_picked_inorm_none_po_kernel(
             second(c)
         for a in range(2):
             drain(nc.scalar.copy, 0, a)
-        store(0)
         second(3)
         for c in range(1, 4):
+            per_pair = len(y_banks[c]) // 2
             for a in range(len(y_banks[c])):
                 drain(nc.scalar.copy, c, a)
-            store(c)
+                if c % 2 == 1 and (a + 1) % per_pair == 0:
+                    store(c // 2, a // per_pair)
         for c in range(4):
-            weave(nc.vector.tensor_copy, y_b[c][:], y[c][:])
+            weave(nc.vector.tensor_copy, y_b[c][:], y[c])
             if c > 0:
                 planes(c - 1)
         planes(3)

@@ -227,6 +227,9 @@ def tile_picked_inorm_none_po_kernel(
                 out_rows[:, 2 * u : 2 * u + 2, h * HALF : (h + 1) * HALF], y_half[h][:, 2 * u : 2 * u + 2, :]
             )
 
+        def store_chunk(c):
+            nc.sync.dma_start(out_rows[:, :, c * CH : (c + 1) * CH], y[c])
+
         def planes(c):
             cols = slice(c * CH, (c + 1) * CH)
             nc.vector.quantize_mx(
@@ -259,13 +262,16 @@ def tile_picked_inorm_none_po_kernel(
             second(c)
         for a in range(2):
             drain(nc.scalar.copy, 0, a)
+        store_chunk(0)
         second(3)
         for c in range(1, 4):
             per_pair = len(y_banks[c]) // 2
             for a in range(len(y_banks[c])):
                 drain(nc.scalar.copy, c, a)
-                if c % 2 == 1 and (a + 1) % per_pair == 0:
+                if c == 3 and (a + 1) % per_pair == 0:
                     store(c // 2, a // per_pair)
+            if c == 1:
+                store_chunk(1)
         for c in range(4):
             weave(nc.vector.tensor_copy, y_b[c][:], y[c])
             if c > 0:

@@ -235,10 +235,10 @@ def tile_picked_inorm_none_po_kernel(
             nc.vector.quantize_mx(
                 out=y_c[:, cols].bitcast(FP8X4), scales=y_s[:, cols], in_=y_b[c][:].rearrange("p n t -> p (n t)")
             )
-            if c % 2 == 1:
-                half = slice((c - 1) * CH, (c + 1) * CH)
-                queue = nc.sync if c == 1 else nc.scalar
-                queue.dma_start(out_words[:, half], y_c[:, half].bitcast(I32))
+            if c != 1:
+                part = slice(CH if c == 2 else c * CH, (c + 1) * CH)
+                queue = nc.sync if c < 3 else nc.scalar
+                queue.dma_start(out_words[:, part], y_c[:, part].bitcast(I32))
 
         nc.vector.tensor_scalar(centred[:], h_chunk(3, 0), mv[:, 3, 0:1], gam[:, 0, 3:4], ALU.subtract, ALU.mult)
         nc.vector.tensor_scalar(z_b[0][:, :, 3], centred[:], rstd[:, 3:4], None, ALU.mult)

@@ -98,14 +98,14 @@ def tile_picked_inorm_none_po_kernel(
         rstd = tile("rstd", [P, PACK], F32, tag="late2")
         coef = tile("coef", [P, PACK, 2], F32)
         zt = [tile("zt%d" % c, [P, PACK, CH], BF16) for c in range(2)]
-        w2_b = tile("w2_b", [P, PACK, P, PACK], BF16, tag="w_b")
-        w2_c = tile("w2_c", [P, H], U32)
+        w2_b = [tile("w2_b0", [P, PACK, 64, PACK], BF16), tile("w2_b1", [P, PACK, 64, PACK], BF16, tag="w_b")]
+        w2_c = tile("w2_c", [P, H], U32, tag="w1_c3")
         w2_s = tile("w2_s", [P, H], U8)
 
         def w2_views(h, order):
             m0, m1 = w2_cuts[h] // PACK, w2_cuts[h + 1] // PACK
             return (
-                w2_b[:].rearrange("p t m j -> " + order)[:, m0:m1],
+                w2_b[m0 // 64][:].rearrange("p t m j -> " + order)[:, m0 % 64 : (m1 - 1) % 64 + 1],
                 w2_raw[h][:].rearrange("p j (m t) -> " + order, t=PACK),
             )
 
@@ -115,7 +115,7 @@ def tile_picked_inorm_none_po_kernel(
                 nc.vector.quantize_mx(
                     out=w2_c[:, cols].bitcast(FP8X4),
                     scales=w2_s[:, cols],
-                    in_=w2_b[:, t, 64 * h : 64 * (h + 1)].rearrange("p m j -> p (m j)"),
+                    in_=w2_b[h][:, t].rearrange("p m j -> p (m j)"),
                 )
 
         widths = [HALF] * PACK

@@ -38,7 +38,7 @@ def tile_picked_inorm_none_po_kernel(
         offsets = sb.tile([P, S // 16], U16, name="offsets")
         xw = tile("xw", [P, T], U32)
         xs = tile("xs", [P, T], U8)
-        w2_cuts = [0, 256, 384, 512]
+        w2_cuts = [0, 192, 352, 512]
         w1_raw = tile("w1_raw", [P, PACK, H], F32)
         w2_raw = [
             tile("w2_raw%d" % h, [P, PACK, w2_cuts[h + 1] - w2_cuts[h]], F32, tag="late" if h == 0 else None)
@@ -102,11 +102,11 @@ def tile_picked_inorm_none_po_kernel(
         w2_c = tile("w2_c", [P, H], U32, tag="w1_c3")
         w2_s = tile("w2_s", [P, H], U8)
 
-        def w2_views(h, order):
-            m0, m1 = w2_cuts[h] // PACK, w2_cuts[h + 1] // PACK
+        def w2_views(h, m0, m1, order):
+            first = w2_cuts[h] // PACK
             return (
                 w2_b[m0 // 64][:].rearrange("p t m j -> " + order)[:, m0 % 64 : (m1 - 1) % 64 + 1],
-                w2_raw[h][:].rearrange("p j (m t) -> " + order, t=PACK),
+                w2_raw[h][:].rearrange("p j (m t) -> " + order, t=PACK)[:, m0 - first : m1 - first],
             )
 
         def quant_w2(h):
@@ -161,11 +161,11 @@ def tile_picked_inorm_none_po_kernel(
 
         for t in range(PACK):
             project(t)
-        nc.scalar.copy(*w2_views(0, "p m j t"))
+        nc.scalar.copy(*w2_views(0, 0, 48, "p m j t"))
         neg_gam = tile("neg_gam", [P, PACK], F32, tag="late")
         nc.scalar.activation(neg_gam[:], gam[:, 0, :], ACT.Copy, scale=-1.0)
-        for h in (1, 2):
-            nc.gpsimd.tensor_scalar(*w2_views(h, "p m t j"), 1.0, 0.0, ALU.mult, ALU.add)
+        for h, m0, m1 in ((1, 48, 64), (1, 64, 88), (2, 88, P)):
+            nc.gpsimd.tensor_scalar(*w2_views(h, m0, m1, "p m t j"), 1.0, 0.0, ALU.mult, ALU.add)
         for t in range(PACK):
             moments(t)
             aggregate(t)

from contextlib import ExitStack

import concourse.mybir as mybir

F32 = mybir.dt.float32
BF16 = mybir.dt.bfloat16
I32 = mybir.dt.int32
U32 = mybir.dt.uint32
U16 = mybir.dt.uint16
U8 = mybir.dt.uint8
FP8X4 = mybir.dt.float8_e4m3fn_x4
ACT = mybir.ActivationFunctionType
ALU = mybir.AluOpType

P = 128
PACK = 4
T = 1024
S = 512
H = 512
HALF = S // 2
CH = S // 4
EPS = 1e-5

FLOPS = 2 * 2 * 512 * 512 * 512


def tile_picked_inorm_none_po_kernel(
    tc, x_words, x_scales, w1, w2, gamma, offs, out_0, out_1, out_2
):
    nc = tc.nc
    with ExitStack() as ctx:
        sb = ctx.enter_context(tc.tile_pool(name="sb", bufs=1))
        ps = ctx.enter_context(tc.psum_pool(name="ps", bufs=1))

        def tile(name, shape, dtype, tag=None):
            return sb.tile(shape, dtype, name=name, tag=tag or name, align_bytes=64)

        offsets = sb.tile([P, S // 16], U16, name="offsets")
        xw = tile("xw", [P, T], U32)
        xs = tile("xs", [P, T], U8)
        w2_cuts = [0, 192, 352, 512]
        w1_raw = tile("w1_raw", [P, PACK, H], F32)
        w2_raw = [
            tile("w2_raw%d" % h, [P, PACK, w2_cuts[h + 1] - w2_cuts[h]], F32, tag="late" if h == 0 else None)
            for h in range(3)
        ]
        warm = tile("warm", [P, 2], F32)

        nc.vector.memset(xs[:].bitcast(I32), 0)
        nc.vector.memset(warm[:, 0:1], 1.0)
        nc.scalar.activation(warm[:, 1:2], warm[:, 0:1], ACT.Abs_reciprocal_sqrt, bias=EPS)

        nc.sync.dma_start(xw[:].bitcast(I32), x_words[0].rearrange("p c r -> p (c r)").bitcast(I32))
        nc.sync.dma_start(offsets[:], offs)
        for q in range(4):
            nc.sync.dma_start(
                xs[32 * q : 32 * q + 4, :].bitcast(I32), x_scales[0, 4 * q : 4 * q + 4, :].bitcast(I32)
            )
        w2_rows = w2.rearrange("(p j) n -> p j n", j=PACK)
        nc.sync.dma_start(w1_raw[:], w1.rearrange("(p j) n -> p j n", j=PACK))
        for h in range(3):
            nc.sync.dma_start(w2_raw[h][:], w2_rows[:, :, w2_cuts[h] : w2_cuts[h + 1]])

        xg = tile("xg", [P, S], U32)
        xsg = tile("xsg", [P, S], U8)
        nc.vector.tensor_copy(xg[:], xw[:].indirect(offsets[:]))
        nc.vector.tensor_copy(xsg[:], xs[:].indirect(offsets[:]))
        gam = tile("gam", [P, 2, PACK], F32, tag="xw")
        nc.scalar.dma_start(gam[:, 0, :], gamma.rearrange("(p t) o -> p (t o)", t=PACK))

        w1_b = tile("w1_b", [P, PACK, P, PACK], BF16, tag="w_b")
        w1_c = [tile("w1_c%d" % t, [P, P], U32) for t in range(PACK)]
        w1_s = [tile("w1_s%d" % t, [P, P], U8) for t in range(PACK)]

        def cast_w1(copy, a, m0, m1):
            copy(
                w1_b[:].rearrange("p t m j -> p m j t")[:, m0:m1, :, 2 * a : 2 * a + 2],
                w1_raw[:].rearrange("p j (m t) -> p m j t", t=PACK)[:, m0:m1, :, 2 * a : 2 * a + 2],
            )

        def quant_w1(t):
            nc.vector.quantize_mx(
                out=w1_c[t][:].bitcast(FP8X4), scales=w1_s[t][:], in_=w1_b[:, t].rearrange("p m j -> p (m j)")
            )

        cast_w1(nc.vector.tensor_copy, 0, 0, 84)
        cast_w1(nc.scalar.copy, 0, 84, P)
        cast_w1(nc.vector.tensor_copy, 1, 0, 40)
        cast_w1(nc.scalar.copy, 1, 80, P)
        quant_w1(0)
        quant_w1(1)
        cast_w1(nc.vector.tensor_copy, 1, 40, 80)
        quant_w1(2)
        quant_w1(3)

        stats = tile("stats", [P, PACK, 12], F32)
        mv = tile("mv", [P, PACK, 2], F32)
        rstd = tile("rstd", [P, PACK], F32, tag="late2")
        coef = tile("coef", [P, PACK, 2], F32)
        zt = [tile("zt%d" % c, [P, PACK, CH], BF16) for c in range(2)]
        w2_b = [tile("w2_b0", [P, PACK, 64, PACK], BF16), tile("w2_b1", [P, PACK, 64, PACK], BF16, tag="w_b")]
        w2_c = tile("w2_c", [P, H], U32, tag="w1_c3")
        w2_s = tile("w2_s", [P, H], U8)

        def w2_views(h, m0, m1, order):
            first = w2_cuts[h] // PACK
            return (
                w2_b[m0 // 64][:].rearrange("p t m j -> " + order)[:, m0 % 64 : (m1 - 1) % 64 + 1],
                w2_raw[h][:].rearrange("p j (m t) -> " + order, t=PACK)[:, m0 - first : m1 - first],
            )

        def quant_w2(h):
            for t in range(PACK):
                cols = slice(t * P + 64 * h, t * P + 64 * (h + 1))
                nc.vector.quantize_mx(
                    out=w2_c[:, cols].bitcast(FP8X4),
                    scales=w2_s[:, cols],
                    in_=w2_b[h][:, t].rearrange("p m j -> p (m j)"),
                )

        widths = [HALF] * PACK
        banks = [[2 * t, 2 * t + 1] for t in range(PACK)]
        hb = [[] for t in range(PACK)]

        def project(t):
            for h, bank in enumerate(banks[t]):
                cols = slice(h * widths[t], (h + 1) * widths[t])
                hb[t].append(ps.tile([P, widths[t]], F32, name="h%d%d" % (t, h), tag="bank%d" % bank))
                nc.tensor.matmul_mx(
                    out=hb[t][h][:],
                    lhsT=w1_c[t][:].bitcast(FP8X4),
                    lhsT_scale=w1_s[t][:],
                    rhs=xg[:, cols].bitcast(FP8X4),
                    rhs_scale=xsg[:, cols],
                    start=True,
                    stop=True,
                )

        def h_chunk(t, c):
            h, c0 = divmod(c * CH, widths[t])
            return hb[t][h][:, c0 : c0 + CH]

        def moments(t):
            for h in range(len(banks[t])):
                nc.vector.bn_stats(stats[:, t, 6 * h : 6 * h + 6], hb[t][h][:])

        def aggregate(t):
            nc.vector.bn_aggr(mv[:, t, :], stats[:, t, 0 : 6 * len(banks[t])])

        def inverse_deviation(t):
            nc.scalar.activation(rstd[:, t : t + 1], mv[:, t, 1:2], ACT.Abs_reciprocal_sqrt, bias=EPS)
            nc.scalar.activation(gam[:, 1, t : t + 1], mv[:, t, 0:1], ACT.Copy, scale=neg_gam[:, t : t + 1])

        def coefficients(t):
            nc.scalar.activation(coef[:, t, :], gam[:, :, t], ACT.Copy, scale=rstd[:, t : t + 1])

        def normalise(t, c):
            nc.scalar.activation(
                zt[c][:, t, :], h_chunk(t, c), ACT.Identity, bias=coef[:, t, 1:2], scale=coef[:, t, 0:1]
            )

        for t in range(PACK):
            project(t)
        nc.scalar.copy(*w2_views(0, 0, 48, "p m j t"))
        neg_gam = tile("neg_gam", [P, PACK], F32, tag="late")
        nc.scalar.activation(neg_gam[:], gam[:, 0, :], ACT.Copy, scale=-1.0)
        for h, m0, m1 in ((1, 48, 64), (1, 64, 88), (2, 88, P)):
            nc.gpsimd.tensor_scalar(*w2_views(h, m0, m1, "p m t j"), 1.0, 0.0, ALU.mult, ALU.add)
        for t in range(PACK):
            moments(t)
            aggregate(t)
            inverse_deviation(t)
            if t > 0:
                normalise(t - 1, 0)
            coefficients(t)
            if t > 0:
                normalise(t - 1, 1)

        def weave(copy, dst, src, t1=PACK):
            copy(
                dst.rearrange("p (c i) t -> p c t i", i=4)[:, :, 0:t1],
                src.rearrange("p t (c i) -> p c t i", i=4)[:, :, 0:t1],
            )

        z_b = [tile("z_b%d" % c, [P, CH, PACK], BF16) for c in range(4)]
        z_c = [tile("z_c%d" % c, [P, CH], U32) for c in range(4)]
        z_s = [tile("z_s%d" % c, [P, CH], U8) for c in range(4)]
        y_half = [tile("y%d" % h, [P, PACK, HALF], F32) for h in range(2)]
        y = [y_half[c // 2][:, :, (c % 2) * CH : (c % 2 + 1) * CH] for c in range(4)]
        y_b = [tile("y_b%d" % c, [P, CH, PACK], BF16) for c in range(4)]
        y_c = tile("y_c", [P, S], U32)
        y_s = tile("y_s", [P, S], U8)
        centred = tile("centred", [P, CH], F32)
        out_rows = out_0.rearrange("(p t) n -> p t n", t=PACK)
        out_words = out_1[0].rearrange("p c r -> p (c r)").bitcast(I32)

        def quant_z(c):
            nc.vector.quantize_mx(
                out=z_c[c][:].bitcast(FP8X4), scales=z_s[c][:], in_=z_b[c][:].rearrange("p n t -> p (n t)")
            )

        y_banks = [[0, 2], [4, 6], [1, 3], [5, 7, 0, 2]]
        acc = [[] for c in range(4)]

        def second(c):
            group = PACK // len(y_banks[c])
            for a, bank in enumerate(y_banks[c]):
                acc[c].append(ps.tile([P, group, CH], F32, name="y%d%d" % (c, a), tag="bank%d" % bank))
                for e in range(group):
                    t = group * a + e
                    nc.tensor.matmul_mx(
                        out=acc[c][a][:, e, :],
                        lhsT=w2_c[:, t * P : (t + 1) * P].bitcast(FP8X4),
                        lhsT_scale=w2_s[:, t * P : (t + 1) * P],
                        rhs=z_c[c][:].bitcast(FP8X4),
                        rhs_scale=z_s[c][:],
                        start=True,
                        stop=True,
                    )

        def drain(copy, c, a):
            group = PACK // len(y_banks[c])
            copy(y[c][:, group * a : group * (a + 1), :], acc[c][a][:])

        def store(h, u):
            nc.sync.dma_start(
                out_rows[:, 2 * u : 2 * u + 2, h * HALF : (h + 1) * HALF], y_half[h][:, 2 * u : 2 * u + 2, :]
            )

        def store_chunk(c):
            nc.sync.dma_start(out_rows[:, :, c * CH : (c + 1) * CH], y[c])

        def planes(c):
            cols = slice(c * CH, (c + 1) * CH)
            nc.vector.quantize_mx(
                out=y_c[:, cols].bitcast(FP8X4), scales=y_s[:, cols], in_=y_b[c][:].rearrange("p n t -> p (n t)")
            )
            if c != 1:
                part = slice(CH if c == 2 else c * CH, (c + 1) * CH)
                queue = nc.sync if c < 3 else nc.scalar
                queue.dma_start(out_words[:, part], y_c[:, part].bitcast(I32))

        nc.vector.tensor_scalar(centred[:], h_chunk(3, 0), mv[:, 3, 0:1], gam[:, 0, 3:4], ALU.subtract, ALU.mult)
        nc.vector.tensor_scalar(z_b[0][:, :, 3], centred[:], rstd[:, 3:4], None, ALU.mult)
        weave(nc.vector.tensor_copy, z_b[0][:], zt[0][:], 3)
        quant_w2(0)
        quant_w2(1)
        normalise(3, 1)
        zt.append(tile("zt2", [P, PACK, CH], BF16, tag="late"))
        zt.append(tile("zt3", [P, PACK, CH], BF16, tag="late2"))
        for c in (2, 3):
            for t in (3, 2, 0, 1):
                normalise(t, c)
        quant_z(0)
        weave(nc.vector.tensor_copy, z_b[1][:], zt[1][:])
        weave(nc.vector.tensor_copy, z_b[2][:], zt[2][:])
        quant_z(1)
        quant_z(2)
        weave(nc.vector.tensor_copy, z_b[3][:], zt[3][:])
        quant_z(3)
        for c in range(3):
            second(c)
        for a in range(2):
            drain(nc.scalar.copy, 0, a)
        store_chunk(0)
        second(3)
        for c in range(1, 4):
            per_pair = len(y_banks[c]) // 2
            for a in range(len(y_banks[c])):
                drain(nc.scalar.copy, c, a)
                if c == 3 and (a + 1) % per_pair == 0:
                    store(c // 2, a // per_pair)
            if c == 1:
                store_chunk(1)
        for c in range(4):
            weave(nc.vector.tensor_copy, y_b[c][:], y[c])
            if c > 0:
                planes(c - 1)
        planes(3)
        for q in range(4):
            queue = nc.sync if q < 3 else nc.scalar
            queue.dma_start(
                out_2[0, 4 * q : 4 * q + 4, :].bitcast(I32), y_s[32 * q : 32 * q + 4, :].bitcast(I32)
            )
